import numpy as np, ml_dtypes
CORES = [23,119,17,113]
N = 4
BF = ml_dtypes.bfloat16
def gentries(a):
    return np.ascontiguousarray(a.reshape(8, 16, -1).transpose(0, 2, 1)).reshape(8, -1)
def gtable(e):
    e = np.asarray(e); return np.ascontiguousarray(e.reshape(8, -1, 16).transpose(0, 2, 1)).reshape(128, -1).astype(np.int32)
W, UN, P, SH, MS = 4096, 256, 16, 5, (1, 2, 3)
def parts(rng):
    e = (0.5 + 2.5 * rng.random((N, 8, 16, 1))).astype(np.float32)
    sh = np.minimum(np.floor(256 * rng.random((N, 8, 16, W), dtype=np.float32) ** e), 255)
    return sh, rng.integers(0, W, (N, 8, UN, P))
def pack(sh, un):
    return {"shelf": np.ascontiguousarray(sh.reshape(N, 128, W)).astype(np.float32).astype(BF), "units": np.stack([gtable(a.reshape(8, -1)) for a in un])}
def setup_inputs(rng):
    sh, un = parts(rng)
    return pack(sh, un)
def setup_inputs_ties(rng):
    sh, un = parts(rng)
    sh = (rng.random((N, 8, 16, W)) < 0.03) * rng.choice(np.array([1, 7, 255]), (1, 8, 1, 1))
    sh[:, rng.integers(0, 8)] = 9
    return pack(sh, un)
def setup_inputs_alike(rng):
    sh, un = parts(rng)
    un[:, 0] = un[0, 0].copy()
    un[:, 1] = rng.choice(np.array([0, 1, W - 1, W // 2]), (N, UN, P))
    un[:, 2] = un[:, 2, :1].copy()
    un[:, 3] = un[:, 3, :, :1].copy()
    un[:, 4] = 0
    un[:, 5, 1::2] = un[:, 5, ::2].copy()
    un[:, 6, :, P // 2:] = un[:1, 6, :1, P // 2:].copy()
    return pack(sh, un)
def setup_inputs_ends(rng):
    sh, un = parts(rng)
    sh[:, :7] = sh[:1, :7].copy(); x = rng.integers(1, W, (N, 7, UN)); un[:, :7] = 0
    for g, e in enumerate((0, P - 1, P // 2 - 1, P // 2, 1, P - 2, int(rng.integers(0, P)))): un[:, g, :, e] = x[:, g]
    return pack(sh, un)
def setup_inputs_rare(rng):
    sh, un = parts(rng)
    few = W // (8 * P) * np.array([1, 2, 3, 4, 2, 3])[:, None, None]
    hit = np.argsort(rng.random((N, 6, 1, W)), axis=-1) < few
    v = rng.integers(1, 256, (N, 6, 16, W)); v[:, 0] = 1; v[:, 1] = 255
    v = np.where(hit, v, 0); v[:, 4:] = 255 - v[:, 4:]
    sh[:, :6] = v
    sh[:, 6] = rng.choice(np.array([0, 1, 2, 253, 254, 255]), (N, 16, W))
    sh[:, 7] = np.clip(rng.integers(-64, 320, (N, 16, W)), 0, 255)
    sh = np.where((sh == 0) & (rng.random(sh.shape, dtype=np.float32) < 0.5), np.float32(-0.0), sh)
    return pack(sh, un)
def setup_inputs_spread(rng):
    sh, un = parts(rng)
    k = np.exp2(8 * rng.random((N, 8, 1, W))) * (rng.random((N, 8, 1, W)) > 0.0625)
    sh = np.minimum(np.floor(rng.random((N, 8, 16, W)) * k), 255)
    un = np.minimum((W * rng.random((N, 8, UN, P)) ** rng.choice(np.array([1, 2, 4, 8]), (N, 8, 1, 1))).astype(np.int64), W - 1)
    return pack(sh, un)
def check_inputs(d):
    bad = []; v = np.asarray(d["shelf"]).astype(np.float32)
    if not np.all((v >= 0) & (v <= 255) & (v == np.floor(v))): bad.append("values of shelf")
    if np.min(d["units"]) < 0 or np.max(d["units"]) > W - 1: bad.append("range of units")
    return bad
def reference(shelf, units):
    tab = np.ascontiguousarray(shelf.astype(np.float32).astype(np.int16).reshape(N, 8, 16, W).transpose(0, 1, 3, 2))
    un = np.stack([gentries(a) for a in units]).astype(np.int64).reshape(N, 8, UN, P)
    A = np.zeros((N, 8), np.int64); rank = np.arange(N); place = np.arange(P)
    n3, g3 = rank[:, None, None], np.arange(8)[None, :, None]
    def measure(x):
        z = (A[:, :, None, None] + np.add.accumulate(x, axis=3)) & 4095
        c = ((z * z >> SH) + x) & (W - 1)
        b = tab[n3[..., None], g3[..., None], c]
        return np.sum((np.max(b, axis=3) - np.min(b, axis=3)).astype(np.int64), axis=3)
    for m in MS:
        mate = rank ^ m; low = (rank < mate)[:, None, None]
        q = measure(un)
        order = np.argsort(np.where(low, -q, q), axis=2, kind="stable")
        own = un[n3, g3, order]; qo = q[n3, g3, order]; far = own[mate]; qf = qo[mate]
        s0 = np.where(low, qo > qf, qf > qo)
        first = np.zeros((N, 8, UN), np.int64); n = P
        while n > 1:
            n = n // 2
            swapped = (place >= first[..., None]) & (place < first[..., None] + n)
            a = measure(np.where(swapped, far, own)); b = a[mate]
            s = np.where(low, a > b, b > a)
            first = np.where(s != s0, first, first + n)
        takes = np.where(low, qo < qf, qo <= qf)
        new = np.where(takes[..., None] & (place == first[..., None]), far, own)
        un = np.zeros_like(un); un[n3, g3, order] = new
        A = np.sum(first, axis=2)
    return {"yu": np.stack([gtable(a.reshape(8, -1)) for a in un]).astype(np.float32), "yq": q.astype(np.float32)}

@@ -1,0 +1,488 @@
+from concourse.mybir import AluOpType as OP, ActivationFunctionType as AF
+
+BCH = [(0, 64), (64, 128), (128, 192), (192, 256)]
+TCH = [(0, 44), (44, 86), (86, 128)]
+SUBS = 2
+NS = 10
+ROUNDS = (1, 2, 3)
+P2 = 2.0 ** -12
+NE = 8
+
+SCRATCH = {}
+for _n, _w, _d in [
+        ("sh", 4096, "bfloat16"), ("sh1", 4096, "bfloat16"), ("sh2", 4096, "bfloat16"), ("sh3", 4096, "bfloat16"), ("uin", 256, "int32"),
+        ("ip", 1, "int32"), ("im", 128, "int32"), ("jj", 1024, "int32"), ("ii", 8, "int32"), ("fc", 24, "float32"), ("mg", 128, "int32"),
+        ("bf", 128, "float32"), ("gef", 128, "float32"), ("trif", 128, "float32"), ("idf", 128, "float32"), ("wa", 128, "float32"),
+        ("mh", 19 * 128, "float16"), ("mb", 13 * 128, "bfloat16"), ("da", 6 * 128, "float16"),
+        ("half", 8, "float16"), ("one", 128, "float16"), ("ones", 256, "bfloat16"), ("mhalf", 64, "bfloat16"), ("tie", 256, "bfloat16"),
+        ("dm", 64, "float32"), ("rm", 1024, "bfloat16"), ("bg", 1024, "bfloat16"), ("bs", 8, "float32"), ("bt", 8, "float32"),
+        ("ac", 16, "float32"), ("xc", 256, "float16"), ("tb", 256, "bfloat16"), ("sq", 256, "float32"), ("yb", 256, "int32"),
+        ("cb", 256, "int32"), ("c16", 256, "uint16"), ("gb", 4096, "bfloat16"), ("mx", 4096, "bfloat16"), ("mn", 4096, "bfloat16"),
+        ("ksb", 256, "float32"), ("kd", 256, "float32"), ("kc", 256, "float32"), ("vu", 256, "int32"), ("acc", 16, "float32"),
+        ("trash", 1024, "bfloat16"), ("cmp", 4096, "bfloat16"), ("cs", 4096, "bfloat16"), ("rl", 48, "uint16"),
+        ("vs", 3 * 272, "int32"), ("vf", 3 * 144, "int32"), ("nx", 3 * 272, "int32"), ("nf", 3 * 144, "int32"),
+        ("oi", 256, "int32"), ("oc", 256, "float16"), ("qo", 128, "int32"), ("qf", 128, "int32"), ("d", 128, "int32"),
+        ("s0", 128, "float32"), ("sg", 4 * 128, "float32"), ("tl", 256, "float32"), ("u", 128, "float32"), ("e", 128, "float32"),
+        ("rr", 128, "float16"), ("r5", 128, "float32"), ("r2", 256, "float32"), ("ns", 256, "int32"), ("cnt", 8, "float32"),
+        ("sgn", 128, "bfloat16"), ("yo", 256, "float32"), ("qi", 256, "int32"), ("qy", 256, "float32")]:
+    SCRATCH[_n] = ("sbuf", [128, _w], _d)
+for _b in range(8):
+    SCRATCH["p%d" % _b] = ("psum", [128, 512], "float32")
+SEMAPHORES = ["eP", "eV", "eS", "eG", "ldu", "lds0", "lds1", "lsem", "styu0", "styu1", "styq"]
+SEMAPHORES += ["v%d" % r for r in range(3)] + ["n%d" % r for r in range(3)] + ["s%d_%d" % (r, h) for r in range(3) for h in range(2)]
+
+CY = 0.00083
+COST = {"V": 0.06, "S": 0.07, "P": 0.03, "lat": 0.18, "self": 0.08, "send": 0.8, "net": 2.6, "netS": 10.0, "g": 1.56, "long": 0.25}
+
+
+def build(rank):
+    ops, hist, bank, stg = [], {}, {}, [None]
+
+    def add(eng, fn, rd, wr, cost, sem=None, amt=1, dep=(), kind="c", lat=None, n=1):
+        i = len(ops)
+        deps = set(dep)
+        for acc, w in [(a, False) for a in rd] + [(a, True) for a in wr]:
+            nm, lo, hi = acc[0], acc[1], acc[2]
+            if nm[0] == "p" and nm[1:].isdigit():
+                st = bank.setdefault(nm, [None, [], []])
+                if st[0] != eng:
+                    st[2] = st[1]
+                    st[1] = []
+                    st[0] = eng
+                deps.update(st[2])
+                st[1].append(i)
+                continue
+            keep = []
+            for (a, b, j, jw) in hist.setdefault(nm, []):
+                over = a < hi and lo < b and j != i
+                if over and (w or jw):
+                    deps.add(j)
+                if not (over and w and lo <= a and b <= hi):
+                    keep.append((a, b, j, jw))
+            keep.append((lo, hi, i, w))
+            hist[nm] = keep
+        deps.discard(i)
+        ops.append({"e": eng, "fn": fn, "d": sorted(deps), "c": cost, "sem": sem, "amt": amt, "k": kind, "lat": lat,
+                    "o": [a[0] for a in wr], "s": stg[0], "n": n})
+        return i
+
+    def A(nm, lo=0, hi=None, st=1):
+        return (nm, lo, SCRATCH[nm][1][1] if hi is None else hi, st)
+
+    def ap(T, a):
+        return T[a[0]][:, a[1]:a[2]:a[3]] if a[3] != 1 else T[a[0]][:, a[1]:a[2]]
+
+    def size(a):
+        return (a[2] - a[1] + a[3] - 1) // a[3]
+
+    def vcost(n, f=1.0):
+        return COST["V"] + max(64, n * f) * CY
+
+    def arg(T, s):
+        return ap(T, s) if isinstance(s, tuple) else s
+
+    def cols(*xs):
+        return [s for s in xs if isinstance(s, tuple)]
+
+    def ts(out, i0, s1, s2, o1, o2=None):
+        def fn(g, T):
+            if o2 is None:
+                return g.vector.tensor_scalar(ap(T, out), ap(T, i0), arg(T, s1), None, o1)
+            return g.vector.tensor_scalar(ap(T, out), ap(T, i0), arg(T, s1), arg(T, s2), o1, o2)
+        return add("V", fn, [i0] + cols(s1, s2), [out], vcost(size(out)))
+
+    def tt(out, i0, i1, op):
+        f = 1 if (i0[0][0] == "p" or i1[0][0] == "p") else 2
+        return add("V", lambda g, T: g.vector.tensor_tensor(ap(T, out), ap(T, i0), ap(T, i1), op), [i0, i1], [out], vcost(size(out), f))
+
+    def cp(out, i0):
+        return add("V", lambda g, T: g.vector.tensor_copy(ap(T, out), ap(T, i0)), [i0], [out], vcost(size(out)))
+
+    def scan(out, d0, d1, o0, o1, f=0.5):
+        return add("V", lambda g, T: g.vector.tensor_tensor_scan(ap(T, out), ap(T, d0), ap(T, d1), 0.0, o0, o1), [d0, d1], [out], vcost(size(out), f))
+
+    def act(out, i0, func, bias=None, scale=None, acc=None):
+        def fn(g, T):
+            kw = {}
+            if bias is not None:
+                kw["bias"] = arg(T, bias)
+            if scale is not None:
+                kw["scale"] = arg(T, scale)
+            if acc is not None:
+                kw["accum_out"] = ap(T, acc)
+            return g.scalar.activation(ap(T, out), ap(T, i0), func, **kw)
+        return add("S", fn, [i0] + cols(bias, scale), [out] + ([acc] if acc else []), COST["S"] + size(out) * CY)
+
+    def mm(terms, first=True, last=True, dep=()):
+        def fn(g, T):
+            r = None
+            for k, (o, l, x) in enumerate(terms):
+                r = g.tensor.matmul(ap(T, o), ap(T, l), ap(T, x), first and k == 0, last and k == len(terms) - 1)
+            return r
+        c = sum(max(64, size(o)) * (4 if l[0] == "wa" else 1) for o, l, x in terms) * 0.0007
+        return add("P", fn, [x for tm in terms for x in tm[1:]], [terms[0][0]], COST["P"] + c, n=len(terms), dep=dep)
+
+    def gath(out, win, off, eng):
+        n = size(out)
+        if eng == "S":
+            return add("S", lambda g, T: g.scalar.activation(ap(T, out), ap(T, win).indirect(ap(T, off)), AF.Copy), [win, off], [out], 0.065 + n * CY * COST["g"])
+        return add("V", lambda g, T: g.vector.tensor_copy(ap(T, out), ap(T, win).indirect(ap(T, off))), [win, off], [out], 0.05 + n * CY * COST["g"])
+
+    def MH(k):
+        return A("mh", 128 * k, 128 * k + 128)
+
+    def MB(k):
+        return A("mb", 128 * k, 128 * k + 128)
+
+    def DA(k):
+        return A("da", 128 * k, 128 * k + 128)
+
+    def FC(k):
+        return A("fc", k, k + 1)
+
+    def iota(out, pat, base, cm, flag=False):
+        def fn(g, T):
+            if flag:
+                return g.iota(ap(T, out), pat, base, cm, allow_small_or_imprecise_dtypes=True)
+            return g.iota(ap(T, out), pat, base, cm)
+        return add("G", fn, [], [out], 0.13 + 2 * size(out) * CY)
+
+    def dma(dst, src, rd, wr, sem, lat):
+        return add("Y", lambda g, T: g.sync.dma_start(dst(T), src(T)), rd, wr, 0.1, sem=sem, amt=16, kind="dma", lat=lat)
+
+    def send(mate, dst, src, here, sem, net, dep=()):
+        i = add("G", (mate, dst, src, sem), [src], [], COST["send"], dep=dep, kind="send")
+        add("N", None, [], [here], 0.0, sem=sem, amt=NE, dep=(i,), kind="net", lat=net)
+        return i
+
+    def send_shelf(r, dep=()):
+        for h in range(2):
+            far = A("sh%d" % (r + 1), 2048 * h, 2048 * h + 2048)
+            send(rank ^ ROUNDS[r], far, A("sh", 2048 * h, 2048 * h + 2048), far, "s%d_%d" % (r, h), COST["netS"] * (h + 1), dep)
+
+    dma(lambda T: T.uin[:], lambda T: T.units[:], [], [A("uin")], "ldu", 2.5)
+    dma(lambda T: T.sh[:, 0:2048], lambda T: T.shelf[:, 0:2048], [], [A("sh", 0, 2048)], "lds0", 5.0)
+    dma(lambda T: T.sh[:, 2048:4096], lambda T: T.shelf[:, 2048:4096], [], [A("sh", 2048, 4096)], "lds1", 8.0)
+    iota(A("ip"), [[1, 1]], 0, 1)
+    iota(A("im"), [[1, 128]], 0, 0)
+    iota(A("jj"), [[0, 64], [1, 16]], 0, 0)
+    iota(A("tie"), [[-1, 256]], 255, 0, True)
+    send_shelf(0)
+    cp(FC(0), A("ip"))
+    ts(A("ii", 0, 1), A("ip"), 4, None, OP.arith_shift_right)
+    cp(FC(1), A("ii", 0, 1))
+    ts(A("ii", 1, 2), A("ip"), 15, None, OP.bitwise_and)
+    cp(FC(2), A("ii", 1, 2))
+    ts(A("mg"), A("im"), 4, None, OP.arith_shift_right)
+    ts(A("bf"), A("mg"), FC(1), None, OP.is_equal)
+    ts(A("gef"), A("im"), FC(0), None, OP.is_ge)
+    tt(A("trif"), A("bf"), A("gef"), OP.mult)
+    ts(A("idf"), A("im"), FC(0), None, OP.is_equal)
+    ts(MH(0), A("trif"), 1.0, None, OP.mult)
+    ts(MH(1), A("idf"), 32.0, None, OP.mult)
+    ts(MH(2), A("idf"), 1.0, None, OP.mult)
+    ts(A("half"), A("im", 0, 8), 0.0, 0.5, OP.mult, OP.add)
+    ts(A("one"), A("im"), 0.0, 1.0, OP.mult, OP.add)
+    ts(DA(0), A("idf"), -2048.0, None, OP.mult)
+    for k, src, f in ((0, "idf", -4096.0), (1, "idf", -8388608.0 + 65536.0), (6, "bf", 1.0), (7, "bf", -1.0), (8, "bf", 256.0),
+                      (9, "bf", -256.0), (10, "bf", 4096.0), (11, "bf", -4096.0), (12, "idf", 1.0)):
+        act(MB(k), A(src), AF.Copy, scale=f)
+    add("V", lambda g, T: g.vector.memset(T.ones[:], 1.0), [], [A("ones")], vcost(128))
+    add("V", lambda g, T: g.vector.memset(T.mhalf[:], -0.5), [], [A("mhalf")], vcost(64))
+    ts(A("rm"), A("jj"), 0, None, OP.is_gt)
+    ts(A("bg"), A("jj"), 0, 256.0, OP.is_equal, OP.mult)
+    ts(A("dm"), A("jj", 0, 64), FC(2), None, OP.is_equal)
+    for t in range(4):
+        ts(A("ii", 2 + t, 3 + t), A("ip"), 8 >> t, None, OP.bitwise_and)
+        ts(FC(3 + t), A("ii", 2 + t, 3 + t), 0, None, OP.is_equal)
+        ts(FC(7 + t), FC(3 + t), -16384.0, 8192.0, OP.mult, OP.add)
+        ts(FC(11 + t), FC(3 + t), 65536.0, -8388608.0 + 65536.0, OP.mult, OP.add)
+        ts(FC(15 + t), FC(3 + t), -1.0, None, OP.mult)
+        ts(MH(3 + t), A("trif"), FC(3 + t), None, OP.mult)
+        ts(MH(7 + t), A("trif"), FC(15 + t), None, OP.mult)
+        ts(MH(11 + t), A("idf"), FC(3 + t), 32.0, OP.mult, OP.mult)
+        ts(MH(15 + t), A("idf"), FC(3 + t), -32.0, OP.mult, OP.mult)
+        act(MB(2 + t), A("idf"), AF.Copy, scale=FC(11 + t))
+    ts(A("wa"), A("bf"), FC(2), 0.5, OP.mult, OP.mult)
+    h1 = A("half", 0, 1)
+
+    def pcol(k):
+        return A("p7", 500 + k, 501 + k)
+    mm([(pcol(0), MH(0), h1)])
+    ts(A("bs", 0, 1), pcol(0), 4096.0, 788480.0, OP.mult, OP.add)
+    ts(A("bt", 0, 1), A("bs", 0, 1), P2, -4095.0 / 8192, OP.mult, OP.add)
+    for t in range(4):
+        mm([(pcol(1 + t), MH(0), h1), (pcol(1 + t), MH(3 + t), h1)])
+    ts(A("bs", 1, 5), A("p7", 501, 505), 4096.0, 788480.0, OP.mult, OP.add)
+    ts(A("bt", 1, 5), A("bs", 1, 5), P2, -4095.0 / 8192, OP.mult, OP.add)
+    ts(A("xc"), A("uin"), -2048.0, None, OP.add)
+    a0 = 264 if rank < (rank ^ ROUNDS[0]) else 7
+    ts(A("vs", a0, a0 + 1), A("ip"), 0.0, -2048.0, OP.mult, OP.add)
+
+    def columns(c, lo, hi, k, pre, xpt):
+        n = hi - lo
+        x, w, xp = A("p%d" % (2 * c), 0, n), A("p%d" % (2 * c + 1), 0, n), A("p%d" % (2 * c + 1), 128, 128 + n)
+        tb = A("tb", lo, hi)
+        mm(pre(x))
+        act(tb, x, AF.Identity, bias=A("bt", k, k + 1), scale=P2)
+        i = mm(pre(w), last=False, dep=(mm(xpt(xp)),))
+        mm([(w, MB(0), tb)], first=False, dep=(i,))
+        act(A("sq", lo, hi), w, AF.Square, bias=A("bs", k, k + 1))
+        tt(A("yb", lo, hi), A("sq", lo, hi), xp, OP.add)
+        ts(A("cb", lo, hi), A("yb", lo, hi), 5, 4095, OP.arith_shift_right, OP.bitwise_and)
+        cp(A("c16", lo, hi), A("cb", lo, hi))
+
+    def gather_scan(parts):
+        for (a, b, win) in parts:
+            gath(A("gb", 16 * a, 16 * b), A(win), A("c16", a, b), "S")
+        for (a, b, win) in parts:
+            m = 16 * (b - a)
+            scan(A("mx", 16 * a, 16 * b), A("rm", 0, m), A("gb", 16 * a, 16 * b), OP.mult, OP.max)
+            scan(A("mn", 16 * a, 16 * b), A("bg", 0, m), A("gb", 16 * a, 16 * b), OP.max, OP.min)
+
+    def ends(nm, a, b):
+        return A(nm, 16 * a + 15, 16 * b, 16)
+
+    for r, m in enumerate(ROUNDS):
+        mate = rank ^ m
+        low = rank < mate
+        for c, (lo, hi) in enumerate(BCH):
+            n = hi - lo
+            stg[0] = 1000 * r + c
+            xs = A("xc", lo, hi)
+            columns(c, lo, hi, 0, lambda x: [(x, MH(0), xs), (x, DA(r), A("one", 0, n))],
+                    lambda x: [(x, MH(1), xs), (x, MB(1), A("ones", 0, n))])
+            st = n // SUBS // 2 * 2
+            cut = [lo + s * st for s in range(SUBS)] + [hi]
+            gather_scan([(cut[s], cut[s + 1], "sh") for s in range(SUBS)])
+            mx, mn = ends("mx", lo, hi), ends("mn", lo, hi)
+            kp, vp = A("p%d" % (2 * c), 128, 128 + n), A("p%d" % (2 * c), 256, 256 + n)
+            mm([(kp, MB(8 if low else 9), mx), (kp, MB(9 if low else 8), mn), (kp, MB(12), A("tie", lo, hi))])
+            mm([(vp, MB(10), mx), (vp, MB(11), mn), (vp, MH(2), xs)])
+            tt(A("kd", lo, hi), kp, A("dm", 0, n), OP.mult)
+            cp(A("ksb", lo, hi), kp)
+            scan(A("kc", lo, hi), A("rm", 0, n), A("kd", lo, hi), OP.mult, OP.add, 1)
+            ts(A("vu", lo, hi), vp, 2048.0, None, OP.add)
+        stg[0] = 1000 * r + 20
+        for j in range(16):
+            kcol = A("kc", 16 * j + 15, 16 * j + 16)
+            if j < NS:
+                act(A("trash", 256 * (j % 4), 256 * (j % 4) + 256), A("ksb"), AF.Sign, bias=kcol, scale=-1.0, acc=A("acc", j, j + 1))
+            else:
+                ts(A("cmp", 256 * j, 256 * j + 256), A("ksb"), kcol, None, OP.is_gt)
+                scan(A("cs", 256 * j, 256 * j + 256), A("ones"), A("cmp", 256 * j, 256 * j + 256), OP.mult, OP.add)
+        ts(A("rl", 16 * r + NS, 16 * r + 16), A("cs", 256 * NS + 255, 4096, 256), 1.0, None, OP.mult)
+        ts(A("rl", 16 * r, 16 * r + NS), A("acc", 0, NS), -0.5, 127.5, OP.mult, OP.add)
+        rl = A("rl", 16 * r, 16 * r + 16)
+        v0 = 272 * r + 8
+        vw = A("vs", v0, v0 + 256)
+        add("V", lambda g, T, vw=vw, rl=rl: g.vector.tensor_copy(ap(T, vw).indirect(ap(T, rl)), T.vu[:]), [rl, A("vu")], [vw], 0.05 + 256 * CY * 3)
+        mine = v0 + (0 if low else 128)
+        f0 = 144 * r
+        x0 = f0 + (1 if low else 0)
+        far = A("vf", f0, f0 + 129)
+        iv = send(mate, far, A("vs", v0 + 128, v0 + 257) if low else A("vs", v0 - 1, v0 + 128), far, "v%d" % r, COST["net"])
+        mv, fv = A("vs", mine, mine + 128), A("vf", x0, x0 + 128)
+        if r < 2:
+            stg[0] = 1000 * r + 21
+            send_shelf(r + 1, (iv,))
+        for c, (a, b) in enumerate(TCH):
+            n = b - a
+            stg[0] = 1000 * r + 100 + c
+            L, H = A("oi", 2 * a, 2 * a + n), A("oi", 2 * a + n, 2 * b)
+            cL, cH = A("oc", 2 * a, 2 * a + n), A("oc", 2 * a + n, 2 * b)
+            ow, fr = (L, H) if low else (H, L)
+            cow, cfr = (cL, cH) if low else (cH, cL)
+            ts(ow, A("vs", mine + a, mine + b), 4095, None, OP.bitwise_and)
+            ts(cow, ow, -2048.0, None, OP.add)
+            ts(fr, A("vf", x0 + a, x0 + b), 4095, None, OP.bitwise_and)
+            ts(cfr, fr, -2048.0, None, OP.add)
+            d = A("d", a, b)
+            tt(d, H, L, OP.subtract)
+            ts(d, d, 4095, None, OP.bitwise_and)
+            ts(A("rr", a, b), d, -2048.0, None, OP.add)
+        stg[0] = 1000 * r + 100
+        ac = A("ac", 4 * r + 2, 4 * r + 3)
+        fa = f0 if low else f0 + 128
+        cp(ac, A("vf", fa, fa + 1))
+        ts(DA(3 + r), A("idf"), ac, None, OP.mult)
+        stg[0] = 1000 * r + 103
+        ts(A("qo"), mv, 12, None, OP.arith_shift_right)
+        ts(A("qf"), fv, 12, None, OP.arith_shift_right)
+        qL, qH = (A("qo"), A("qf")) if low else (A("qf"), A("qo"))
+        tt(A("s0"), qL, qH, OP.is_gt)
+        ts(A("s0"), A("s0"), 2.0, -1.0, OP.mult, OP.add)
+        for t in range(4):
+            stg[0] = 1000 * r + 103 + 4 * t
+            ts(A("sg", 128 * t, 128 * t + 128), A("s0"), FC(7 + t), None, OP.mult)
+        tt(A("tl", 0, 128), qL, qH, OP.is_lt)
+        ts(A("tl", 128, 256), A("tl", 0, 128), -1.0, None, OP.add)
+        if r == 2:
+            ts(A("qi"), A("vu"), 12, None, OP.arith_shift_right)
+            cp(A("qy"), A("qi"))
+            dma(lambda T: T.yq[:], lambda T: T.qy[0:128:16, :], [A("qy")], [], "styq", 2.0)
+        dL, dH = (DA(r), DA(3 + r)) if low else (DA(3 + r), DA(r))
+        wL, wH = ("sh", "sh%d" % (r + 1)) if low else ("sh%d" % (r + 1), "sh")
+        for t in range(4):
+            for c, (a, b) in enumerate(TCH):
+                n = b - a
+                lo, mid, hi = 2 * a, 2 * a + n, 2 * b
+                stg[0] = 1000 * r + 100 + 4 * t + c
+                R, oc, one = A("rr", a, b), A("oc", lo, hi), A("one", 0, n)
+
+                def lh(x):
+                    return (x[0], x[1], x[1] + n, 1), (x[0], x[1] + n, x[1] + 2 * n, 1)
+                columns(c, lo, hi, 1 + t,
+                        lambda x: [(x, MH(0), oc), (lh(x)[0], dL, one), (lh(x)[1], dH, one), (lh(x)[0], MH(3 + t), R), (lh(x)[1], MH(7 + t), R)],
+                        lambda x: [(x, MH(1), oc), (x, MB(2 + t), A("ones", 0, 2 * n)), (lh(x)[0], MH(11 + t), R), (lh(x)[1], MH(15 + t), R)])
+                gather_scan([(lo, mid, wL), (mid, hi, wH)])
+                q = A("p%d" % (2 * c), 128, 128 + n)
+                mm([(q, MB(6), ends("mx", lo, mid)), (q, MB(7), ends("mn", lo, mid)), (q, MB(7), ends("mx", mid, hi)),
+                    (q, MB(6), ends("mn", mid, hi)), (q, MB(12), A("mhalf", 0, n))])
+                stg[0] += 4
+                u, e = A("u", a, b), A("e", a, b)
+                tt(u, q, A("sg", 128 * t + a, 128 * t + b), OP.mult)
+                tt(e, A("d" if t == 0 else "e", a, b), u, OP.min)
+                if t < 3:
+                    ts(R, e, 0.0, -2048.0, OP.max, OP.add)
+                    continue
+                if r < 2:
+                    act(A("sgn", a, b), e, AF.Sign, bias=0.5, acc=A("cnt", c, c + 1))
+                r5, rL, rH = A("r5", a, b), A("r2", lo, mid), A("r2", mid, hi)
+                ts(r5, e, 0.0, None, OP.max)
+                tt(rL, r5, A("tl", a, b), OP.mult)
+                tt(rH, r5, A("tl", 128 + a, 128 + b), OP.mult)
+                tt(A("ns", lo, hi), A("oi", lo, hi), A("r2", lo, hi), OP.add)
+                sL, sH = A("ns", lo, mid), A("ns", mid, hi)
+                so, sf = (sL, sH) if low else (sH, sL)
+                ts(A("nf", x0 + a, x0 + b), sf, 4095, None, OP.bitwise_and)
+                ts(A("nx", mine + a, mine + b), so, 4095, None, OP.bitwise_and)
+        stg[0] = 1000 * r + 200
+        nw = A("nx", v0, v0 + 256)
+        n0 = 144 * r
+        if r < 2:
+            pa = A("p0", 500, 501)
+            mm([(pa, A("wa"), A("cnt", c, c + 1)) for c in range(len(TCH))])
+            fcol = n0 if low else n0 + 128
+            ts(A("nf", fcol, fcol + 1), pa, 7680.0, None, OP.add)
+            ts(A("ac", 4 * r, 4 * r + 1), pa, 5632.0, None, OP.add)
+            front, back = A("nx", v0 - 1, v0 + 128), A("nx", v0 + 128, v0 + 257)
+            send(mate, front if low else back, A("nf", n0, n0 + 129), back if low else front, "n%d" % r, COST["net"])
+            rcv = A("nx", v0 + 256, v0 + 257) if low else A("nx", v0 - 1, v0)
+            asum = A("ac", 4 * r + 1, 4 * r + 2)
+            tt(asum, A("ac", 4 * r, 4 * r + 1), rcv, OP.add)
+            ts(DA(r + 1), A("idf"), asum, None, OP.mult)
+            vn = 272 * (r + 1) + 8
+            acol = A("vs", vn + 256, vn + 257) if rank < (rank ^ ROUNDS[r + 1]) else A("vs", vn - 1, vn)
+            cp(acol, asum)
+            add("V", lambda g, T, rl=rl, nw=nw: g.vector.tensor_scalar(T.xc[:], ap(T, nw).indirect(ap(T, rl)), -2048.0, None, OP.add), [rl, nw], [A("xc")], 0.05 + 256 * CY * COST["g"])
+        else:
+            front, back = A("nx", v0, v0 + 128), A("nx", v0 + 128, v0 + 256)
+            send(mate, front if low else back, A("nf", x0, x0 + 128), back if low else front, "n%d" % r, COST["net"])
+            for h in range(2):
+                a, b = 128 * h, 128 * h + 128
+                gath(A("yo", a, b), nw, A("rl", 16 * r + 8 * h, 16 * r + 8 * h + 8), "V")
+                dma(lambda T, a=a, b=b: T.yu[:, a:b], lambda T, a=a, b=b: T.yo[:, a:b], [A("yo", a, b)], [], "styu%d" % h, 2.0)
+    return ops
+
+
+def schedule(ops):
+    n = len(ops)
+    succ = [[] for _ in ops]
+    for i, o in enumerate(ops):
+        for j in o["d"]:
+            succ[j].append(i)
+
+    def lat(j, i):
+        if ops[j]["lat"] is not None:
+            return ops[j]["lat"]
+        return COST["self"] if ops[j]["e"] == ops[i]["e"] else COST["lat"]
+    pr = [0.0] * n
+    sg = [9999 if o["s"] is None else o["s"] for o in ops]
+    for i in range(n - 1, -1, -1):
+        pr[i] = ops[i]["c"] + max([pr[s] + lat(i, s) for s in succ[i]] + [0.0])
+        if ops[i]["s"] is None:
+            sg[i] = min([sg[x] for x in succ[i]] + [9999])
+    cnt = [len(o["d"]) for o in ops]
+    ready, start = [0.0] * n, [0.0] * n
+    free, avail, order = {}, {}, []
+    for i in range(n):
+        if cnt[i] == 0:
+            avail.setdefault(ops[i]["e"], []).append(i)
+    while len(order) < n:
+        best = None
+        for e, lst in avail.items():
+            if not lst:
+                continue
+            f = free.get(e, 0.0)
+            s0 = max(f, min(ready[k] for k in lst))
+            if e == "N":
+                i = min(lst, key=lambda k: ready[k])
+                s = ready[i]
+            else:
+                i = min((k for k in lst if ready[k] <= s0 + 0.02), key=lambda k: (ops[k]["c"] > COST["long"], sg[k], -pr[k]))
+                s = max(f, ready[i])
+            if best is None or s < best[0]:
+                best = (s, i, e)
+        s, i, e = best
+        avail[e].remove(i)
+        start[i] = s
+        end = s + ops[i]["c"]
+        if e != "N":
+            free[e] = end
+        order.append(i)
+        for k in succ[i]:
+            ready[k] = max(ready[k], end + lat(i, k))
+            cnt[k] -= 1
+            if cnt[k] == 0:
+                avail.setdefault(ops[k]["e"], []).append(k)
+    return order, start
+
+
+def rank_program(g, core, T, topo):
+    rank = T.rank_of(core)
+    if rank is None:
+        return
+    ops = build(rank)
+    order, start = schedule(ops)
+    queue = {"P": g.tensor, "V": g.vector, "S": g.scalar, "G": g, "Y": g.sync}
+    own = {"P": "eP", "V": "eV", "S": "eS", "G": "eG"}
+    known = {e: {} for e in queue}
+    after = {}
+    count, sent = {}, 0
+    for i in order:
+        o = ops[i]
+        e = o["e"]
+        if e == "N":
+            o["at"] = (o["sem"], o["amt"])
+            after[i] = {o["sem"]: o["amt"]}
+            continue
+        kn = known[e]
+        need = [ops[j]["at"] + (j,) for j in o["d"]
+                if (e, ops[j]["e"]) != ("P", "P") and kn.get(ops[j]["at"][0], 0) < ops[j]["at"][1]]
+        for (s, v, j) in need:
+            if not any(j2 != j and after[j2].get(s, 0) >= v and (s2 != s or v2 > v or j2 > j) for (s2, v2, j2) in need):
+                queue[e].wait_ge(T.sem[s], v)
+        for (s, v, j) in need:
+            for s2, v2 in after[j].items():
+                kn[s2] = max(kn.get(s2, 0), v2)
+        if o["k"] == "send":
+            mate, dst, src, sem = o["fn"]
+            to = T.cores[mate]
+            rid, pid, ring = topo.addr(to)
+            eng = topo.engines(core, to)[:NE]
+            g.remote_dma(T[dst[0]][:, dst[1]:dst[2]], T[src[0]][:, src[1]:src[2]], T.sem[sem], T.sem.lsem, pid, rid, sum(1 << x for x in eng))
+            sent += len(eng)
+            after[i] = dict(kn)
+            o["at"] = ("lsem", 0)
+            continue
+        s = o["sem"] or own[e]
+        o["fn"](g, T).then_inc(T.sem[s], o["amt"])
+        count[s] = count.get(s, 0) + o["amt"]
+        o["at"] = (s, count[s])
+        after[i] = dict(kn)
+        after[i][s] = count[s]
+    for s, v in sorted(count.items()):
+        if known["G"].get(s, 0) < v:
+            g.wait_ge(T.sem[s], v)
+    g.wait_ge(T.sem.lsem, sent)

@@ -28,11 +28,12 @@ for _n, _w, _d in [
     SCRATCH[_n] = ("sbuf", [128, _w], _d)
 for _b in range(8):
     SCRATCH["p%d" % _b] = ("psum", [128, 512], "float32")
-SEMAPHORES = ["eP", "eV", "eS", "eG", "ldu", "lds0", "lds1", "lsem", "styu0", "styu1", "styq"]
-SEMAPHORES += ["v%d" % r for r in range(3)] + ["n%d" % r for r in range(3)] + ["s%d_%d" % (r, h) for r in range(3) for h in range(2)]
+SEMAPHORES = ["eP", "eV", "eS", "eG", "ldu", "lds0", "lds1", "lds2", "lds3", "lsem", "styu0", "styu1", "styq"]
+SEMAPHORES += ["v%d" % r for r in range(3)] + ["n%d" % r for r in range(3)] + ["s0_%d" % h for h in range(4)] + ["s1_0", "s2_0"]
 
 CY = 0.00083
-COST = {"V": 0.06, "S": 0.07, "P": 0.03, "lat": 0.18, "self": 0.08, "send": 0.8, "net": 2.6, "netS": 10.0, "g": 1.56, "long": 0.25}
+COST = {"V": 0.0302, "S": 0.0645, "P": 0.0405, "lat": 0.161, "self": 0.0428, "send": 0.8, "net": 2.6, "g": 1.8198, "long": 0.2036}
+WIN = 0.0124
 
 
 def build(rank):
@@ -155,19 +156,20 @@ def build(rank):
         add("N", None, [], [here], 0.0, sem=sem, amt=NE, dep=(i,), kind="net", lat=net)
         return i
 
-    def send_shelf(r, dep=()):
-        for h in range(2):
-            far = A("sh%d" % (r + 1), 2048 * h, 2048 * h + 2048)
-            send(rank ^ ROUNDS[r], far, A("sh", 2048 * h, 2048 * h + 2048), far, "s%d_%d" % (r, h), COST["netS"] * (h + 1), dep)
+    def send_shelf(r, cuts, net, dep=()):
+        for h, (a, b) in enumerate(cuts):
+            far = A("sh%d" % (r + 1), a, b)
+            send(rank ^ ROUNDS[r], far, A("sh", a, b), far, "s%d_%d" % (r, a // 1024), net + 3 * h, dep)
 
     dma(lambda T: T.uin[:], lambda T: T.units[:], [], [A("uin")], "ldu", 2.5)
-    dma(lambda T: T.sh[:, 0:2048], lambda T: T.shelf[:, 0:2048], [], [A("sh", 0, 2048)], "lds0", 5.0)
-    dma(lambda T: T.sh[:, 2048:4096], lambda T: T.shelf[:, 2048:4096], [], [A("sh", 2048, 4096)], "lds1", 8.0)
+    for h in range(4):
+        a, b = 1024 * h, 1024 * h + 1024
+        dma(lambda T, a=a, b=b: T.sh[:, a:b], lambda T, a=a, b=b: T.shelf[:, a:b], [], [A("sh", a, b)], "lds%d" % h, 3.5 + 1.5 * h)
     iota(A("ip"), [[1, 1]], 0, 1)
     iota(A("im"), [[1, 128]], 0, 0)
     iota(A("jj"), [[0, 64], [1, 16]], 0, 0)
     iota(A("tie"), [[-1, 256]], 255, 0, True)
-    send_shelf(0)
+    send_shelf(0, [(0, 1024), (1024, 2048), (2048, 3072)], 8.0)
     cp(FC(0), A("ip"))
     ts(A("ii", 0, 1), A("ip"), 4, None, OP.arith_shift_right)
     cp(FC(1), A("ii", 0, 1))
@@ -219,14 +221,17 @@ def build(rank):
     a0 = 264 if rank < (rank ^ ROUNDS[0]) else 7
     ts(A("vs", a0, a0 + 1), A("ip"), 0.0, -2048.0, OP.mult, OP.add)
 
-    def columns(c, lo, hi, k, pre, xpt):
+    def columns(c, lo, hi, k, pre, late, xpt):
         n = hi - lo
-        x, w, xp = A("p%d" % (2 * c), 0, n), A("p%d" % (2 * c + 1), 0, n), A("p%d" % (2 * c + 1), 128, 128 + n)
+        x, w, xp = A("p%d" % (2 * c), 0, n), A("p%d" % (2 * c + 1), 0, n), A("p%d" % (2 * c), 384, 384 + n)
         tb = A("tb", lo, hi)
-        mm(pre(x))
-        act(tb, x, AF.Identity, bias=A("bt", k, k + 1), scale=P2)
-        i = mm(pre(w), last=False, dep=(mm(xpt(xp)),))
+        i = mm(pre(x), last=not late(x))
+        if late(x):
+            i = mm(late(x), first=False, dep=(i,))
+        i = mm(pre(w) + late(w), last=False, dep=(i,))
+        ts(tb, x, P2, A("bt", k, k + 1), OP.mult, OP.add)
         mm([(w, MB(0), tb)], first=False, dep=(i,))
+        mm(xpt(xp))
         act(A("sq", lo, hi), w, AF.Square, bias=A("bs", k, k + 1))
         tt(A("yb", lo, hi), A("sq", lo, hi), xp, OP.add)
         ts(A("cb", lo, hi), A("yb", lo, hi), 5, 4095, OP.arith_shift_right, OP.bitwise_and)
@@ -250,13 +255,13 @@ def build(rank):
             n = hi - lo
             stg[0] = 1000 * r + c
             xs = A("xc", lo, hi)
-            columns(c, lo, hi, 0, lambda x: [(x, MH(0), xs), (x, DA(r), A("one", 0, n))],
+            columns(c, lo, hi, 0, lambda x: [(x, MH(0), xs), (x, DA(r), A("one", 0, n))], lambda x: [],
                     lambda x: [(x, MH(1), xs), (x, MB(1), A("ones", 0, n))])
             st = n // SUBS // 2 * 2
             cut = [lo + s * st for s in range(SUBS)] + [hi]
             gather_scan([(cut[s], cut[s + 1], "sh") for s in range(SUBS)])
             mx, mn = ends("mx", lo, hi), ends("mn", lo, hi)
-            kp, vp = A("p%d" % (2 * c), 128, 128 + n), A("p%d" % (2 * c), 256, 256 + n)
+            kp, vp = A("p%d" % (2 * c + 1), 128, 128 + n), A("p%d" % (2 * c + 1), 256, 256 + n)
             mm([(kp, MB(8 if low else 9), mx), (kp, MB(9 if low else 8), mn), (kp, MB(12), A("tie", lo, hi))])
             mm([(vp, MB(10), mx), (vp, MB(11), mn), (vp, MH(2), xs)])
             tt(A("kd", lo, hi), kp, A("dm", 0, n), OP.mult)
@@ -283,9 +288,11 @@ def build(rank):
         far = A("vf", f0, f0 + 129)
         iv = send(mate, far, A("vs", v0 + 128, v0 + 257) if low else A("vs", v0 - 1, v0 + 128), far, "v%d" % r, COST["net"])
         mv, fv = A("vs", mine, mine + 128), A("vf", x0, x0 + 128)
+        stg[0] = 1000 * r + 21
+        if r == 0:
+            send_shelf(0, [(3072, 4096)], 6.0, (iv,))
         if r < 2:
-            stg[0] = 1000 * r + 21
-            send_shelf(r + 1, (iv,))
+            send_shelf(r + 1, [(0, 4096)], 16.0, (len(ops) - 2,))
         for c, (a, b) in enumerate(TCH):
             n = b - a
             stg[0] = 1000 * r + 100 + c
@@ -333,12 +340,13 @@ def build(rank):
                 def lh(x):
                     return (x[0], x[1], x[1] + n, 1), (x[0], x[1] + n, x[1] + 2 * n, 1)
                 columns(c, lo, hi, 1 + t,
-                        lambda x: [(x, MH(0), oc), (lh(x)[0], dL, one), (lh(x)[1], dH, one), (lh(x)[0], MH(3 + t), R), (lh(x)[1], MH(7 + t), R)],
+                        lambda x: [(x, MH(0), oc), (lh(x)[0], dL, one), (lh(x)[1], dH, one)],
+                        lambda x: [(lh(x)[0], MH(3 + t), R), (lh(x)[1], MH(7 + t), R)],
                         lambda x: [(x, MH(1), oc), (x, MB(2 + t), A("ones", 0, 2 * n)), (lh(x)[0], MH(11 + t), R), (lh(x)[1], MH(15 + t), R)])
                 gather_scan([(lo, mid, wL), (mid, hi, wH)])
-                q = A("p%d" % (2 * c), 128, 128 + n)
-                mm([(q, MB(6), ends("mx", lo, mid)), (q, MB(7), ends("mn", lo, mid)), (q, MB(7), ends("mx", mid, hi)),
-                    (q, MB(6), ends("mn", mid, hi)), (q, MB(12), A("mhalf", 0, n))])
+                q = A("p%d" % (2 * c + 1), 128, 128 + n)
+                i = mm([(q, MB(12), A("mhalf", 0, n)), (q, MB(6), ends("mx", lo, mid)), (q, MB(7), ends("mn", lo, mid))], last=False)
+                mm([(q, MB(7), ends("mx", mid, hi)), (q, MB(6), ends("mn", mid, hi))], first=False, dep=(i,))
                 stg[0] += 4
                 u, e = A("u", a, b), A("e", a, b)
                 tt(u, q, A("sg", 128 * t + a, 128 * t + b), OP.mult)
@@ -362,7 +370,8 @@ def build(rank):
         n0 = 144 * r
         if r < 2:
             pa = A("p0", 500, 501)
-            mm([(pa, A("wa"), A("cnt", c, c + 1)) for c in range(len(TCH))])
+            cn = [(pa, A("wa"), A("cnt", c, c + 1)) for c in range(len(TCH))]
+            mm(cn[-1:], first=False, dep=(mm(cn[:-1], last=False),))
             fcol = n0 if low else n0 + 128
             ts(A("nf", fcol, fcol + 1), pa, 7680.0, None, OP.add)
             ts(A("ac", 4 * r, 4 * r + 1), pa, 5632.0, None, OP.add)
@@ -375,7 +384,11 @@ def build(rank):
             vn = 272 * (r + 1) + 8
             acol = A("vs", vn + 256, vn + 257) if rank < (rank ^ ROUNDS[r + 1]) else A("vs", vn - 1, vn)
             cp(acol, asum)
-            add("V", lambda g, T, rl=rl, nw=nw: g.vector.tensor_scalar(T.xc[:], ap(T, nw).indirect(ap(T, rl)), -2048.0, None, OP.add), [rl, nw], [A("xc")], 0.05 + 256 * CY * COST["g"])
+            for c, (lo, hi) in enumerate(BCH):
+                stg[0] = 1000 * (r + 1) + c
+                xs, rc = A("xc", lo, hi), A("rl", 16 * r + lo // 16, 16 * r + hi // 16)
+                add("V", lambda g, T, xs=xs, rc=rc, nw=nw: g.vector.tensor_scalar(ap(T, xs), ap(T, nw).indirect(ap(T, rc)), -2048.0, None, OP.add),
+                    [rc, nw], [xs], 0.05 + (hi - lo) * CY * COST["g"])
         else:
             front, back = A("nx", v0, v0 + 128), A("nx", v0 + 128, v0 + 256)
             send(mate, front if low else back, A("nf", x0, x0 + 128), back if low else front, "n%d" % r, COST["net"])
@@ -420,7 +433,7 @@ def schedule(ops):
                 i = min(lst, key=lambda k: ready[k])
                 s = ready[i]
             else:
-                i = min((k for k in lst if ready[k] <= s0 + 0.02), key=lambda k: (ops[k]["c"] > COST["long"], sg[k], -pr[k]))
+                i = min((k for k in lst if ready[k] <= s0 + WIN), key=lambda k: (ops[k]["c"] > COST["long"], sg[k], -pr[k]))
                 s = max(f, ready[i])
             if best is None or s < best[0]:
                 best = (s, i, e)
@@ -470,7 +483,7 @@ def rank_program(g, core, T, topo):
             mate, dst, src, sem = o["fn"]
             to = T.cores[mate]
             rid, pid, ring = topo.addr(to)
-            eng = topo.engines(core, to)[:NE]
+            eng = topo.engines(core, to)[-NE:]
             g.remote_dma(T[dst[0]][:, dst[1]:dst[2]], T[src[0]][:, src[1]:src[2]], T.sem[sem], T.sem.lsem, pid, rid, sum(1 << x for x in eng))
             sent += len(eng)
             after[i] = dict(kn)

from concourse.mybir import AluOpType as OP, ActivationFunctionType as AF

BCH = [(0, 64), (64, 128), (128, 192), (192, 256)]
TCH = [(0, 44), (44, 86), (86, 128)]
SUBS = 2
NS = 10
ROUNDS = (1, 2, 3)
P2 = 2.0 ** -12
NE = 8

SCRATCH = {}
for _n, _w, _d in [
        ("sh", 4096, "bfloat16"), ("sh1", 4096, "bfloat16"), ("sh2", 4096, "bfloat16"), ("sh3", 4096, "bfloat16"), ("uin", 256, "int32"),
        ("ip", 1, "int32"), ("im", 128, "int32"), ("jj", 1024, "int32"), ("ii", 8, "int32"), ("fc", 24, "float32"), ("mg", 128, "int32"),
        ("bf", 128, "float32"), ("gef", 128, "float32"), ("trif", 128, "float32"), ("idf", 128, "float32"), ("wa", 128, "float32"),
        ("mh", 19 * 128, "float16"), ("mb", 13 * 128, "bfloat16"), ("da", 6 * 128, "float16"),
        ("half", 8, "float16"), ("one", 128, "float16"), ("ones", 256, "bfloat16"), ("mhalf", 64, "bfloat16"), ("tie", 256, "bfloat16"),
        ("dm", 64, "float32"), ("rm", 1024, "bfloat16"), ("bg", 1024, "bfloat16"), ("bs", 8, "float32"), ("bt", 8, "float32"),
        ("ac", 16, "float32"), ("xc", 256, "float16"), ("tb", 256, "bfloat16"), ("sq", 256, "float32"), ("yb", 256, "int32"),
        ("cb", 256, "int32"), ("c16", 256, "uint16"), ("gb", 4096, "bfloat16"), ("mx", 4096, "bfloat16"), ("mn", 4096, "bfloat16"),
        ("ksb", 256, "float32"), ("kd", 256, "float32"), ("kc", 256, "float32"), ("vu", 256, "int32"), ("acc", 16, "float32"),
        ("trash", 1024, "bfloat16"), ("cmp", 4096, "bfloat16"), ("cs", 4096, "bfloat16"), ("rl", 48, "uint16"),
        ("vs", 3 * 272, "int32"), ("vf", 3 * 144, "int32"), ("nx", 3 * 272, "int32"), ("nf", 3 * 144, "int32"),
        ("oi", 256, "int32"), ("oc", 256, "float16"), ("qo", 128, "int32"), ("qf", 128, "int32"), ("d", 128, "int32"),
        ("s0", 128, "float32"), ("sg", 4 * 128, "float32"), ("tl", 256, "float32"), ("u", 128, "float32"), ("e", 128, "float32"),
        ("rr", 128, "float16"), ("r5", 128, "float32"), ("r2", 256, "float32"), ("ns", 256, "int32"), ("cnt", 8, "float32"),
        ("sgn", 128, "bfloat16"), ("yo", 256, "float32"), ("qi", 256, "int32"), ("qy", 256, "float32")]:
    SCRATCH[_n] = ("sbuf", [128, _w], _d)
for _b in range(8):
    SCRATCH["p%d" % _b] = ("psum", [128, 512], "float32")
SEMAPHORES = ["eP", "eV", "eS", "eG", "ldu", "lds0", "lds1", "lds2", "lds3", "lsem", "styu0", "styu1", "styq"]
SEMAPHORES += ["v%d" % r for r in range(3)] + ["n%d" % r for r in range(3)] + ["s0_%d" % h for h in range(4)] + ["s1_0", "s2_0"]

CY = 0.00083
COST = {"V": 0.0302, "S": 0.0645, "P": 0.0405, "lat": 0.161, "self": 0.0428, "send": 0.8, "net": 2.6, "g": 1.8198, "long": 0.2036}
WIN = 0.0124


def build(rank):
    ops, hist, bank, stg = [], {}, {}, [None]

    def add(eng, fn, rd, wr, cost, sem=None, amt=1, dep=(), kind="c", lat=None, n=1):
        i = len(ops)
        deps = set(dep)
        for acc, w in [(a, False) for a in rd] + [(a, True) for a in wr]:
            nm, lo, hi = acc[0], acc[1], acc[2]
            if nm[0] == "p" and nm[1:].isdigit():
                st = bank.setdefault(nm, [None, [], []])
                if st[0] != eng:
                    st[2] = st[1]
                    st[1] = []
                    st[0] = eng
                deps.update(st[2])
                st[1].append(i)
                continue
            keep = []
            for (a, b, j, jw) in hist.setdefault(nm, []):
                over = a < hi and lo < b and j != i
                if over and (w or jw):
                    deps.add(j)
                if not (over and w and lo <= a and b <= hi):
                    keep.append((a, b, j, jw))
            keep.append((lo, hi, i, w))
            hist[nm] = keep
        deps.discard(i)
        ops.append({"e": eng, "fn": fn, "d": sorted(deps), "c": cost, "sem": sem, "amt": amt, "k": kind, "lat": lat,
                    "o": [a[0] for a in wr], "s": stg[0], "n": n})
        return i

    def A(nm, lo=0, hi=None, st=1):
        return (nm, lo, SCRATCH[nm][1][1] if hi is None else hi, st)

    def ap(T, a):
        return T[a[0]][:, a[1]:a[2]:a[3]] if a[3] != 1 else T[a[0]][:, a[1]:a[2]]

    def size(a):
        return (a[2] - a[1] + a[3] - 1) // a[3]

    def vcost(n, f=1.0):
        return COST["V"] + max(64, n * f) * CY

    def arg(T, s):
        return ap(T, s) if isinstance(s, tuple) else s

    def cols(*xs):
        return [s for s in xs if isinstance(s, tuple)]

    def ts(out, i0, s1, s2, o1, o2=None):
        def fn(g, T):
            if o2 is None:
                return g.vector.tensor_scalar(ap(T, out), ap(T, i0), arg(T, s1), None, o1)
            return g.vector.tensor_scalar(ap(T, out), ap(T, i0), arg(T, s1), arg(T, s2), o1, o2)
        return add("V", fn, [i0] + cols(s1, s2), [out], vcost(size(out)))

    def tt(out, i0, i1, op):
        f = 1 if (i0[0][0] == "p" or i1[0][0] == "p") else 2
        return add("V", lambda g, T: g.vector.tensor_tensor(ap(T, out), ap(T, i0), ap(T, i1), op), [i0, i1], [out], vcost(size(out), f))

    def cp(out, i0):
        return add("V", lambda g, T: g.vector.tensor_copy(ap(T, out), ap(T, i0)), [i0], [out], vcost(size(out)))

    def scan(out, d0, d1, o0, o1, f=0.5):
        return add("V", lambda g, T: g.vector.tensor_tensor_scan(ap(T, out), ap(T, d0), ap(T, d1), 0.0, o0, o1), [d0, d1], [out], vcost(size(out), f))

    def act(out, i0, func, bias=None, scale=None, acc=None):
        def fn(g, T):
            kw = {}
            if bias is not None:
                kw["bias"] = arg(T, bias)
            if scale is not None:
                kw["scale"] = arg(T, scale)
            if acc is not None:
                kw["accum_out"] = ap(T, acc)
            return g.scalar.activation(ap(T, out), ap(T, i0), func, **kw)
        return add("S", fn, [i0] + cols(bias, scale), [out] + ([acc] if acc else []), COST["S"] + size(out) * CY)

    def mm(terms, first=True, last=True, dep=()):
        def fn(g, T):
            r = None
            for k, (o, l, x) in enumerate(terms):
                r = g.tensor.matmul(ap(T, o), ap(T, l), ap(T, x), first and k == 0, last and k == len(terms) - 1)
            return r
        c = sum(max(64, size(o)) * (4 if l[0] == "wa" else 1) for o, l, x in terms) * 0.0007
        return add("P", fn, [x for tm in terms for x in tm[1:]], [terms[0][0]], COST["P"] + c, n=len(terms), dep=dep)

    def gath(out, win, off, eng):
        n = size(out)
        if eng == "S":
            return add("S", lambda g, T: g.scalar.activation(ap(T, out), ap(T, win).indirect(ap(T, off)), AF.Copy), [win, off], [out], 0.065 + n * CY * COST["g"])
        return add("V", lambda g, T: g.vector.tensor_copy(ap(T, out), ap(T, win).indirect(ap(T, off))), [win, off], [out], 0.05 + n * CY * COST["g"])

    def MH(k):
        return A("mh", 128 * k, 128 * k + 128)

    def MB(k):
        return A("mb", 128 * k, 128 * k + 128)

    def DA(k):
        return A("da", 128 * k, 128 * k + 128)

    def FC(k):
        return A("fc", k, k + 1)

    def iota(out, pat, base, cm, flag=False):
        def fn(g, T):
            if flag:
                return g.iota(ap(T, out), pat, base, cm, allow_small_or_imprecise_dtypes=True)
            return g.iota(ap(T, out), pat, base, cm)
        return add("G", fn, [], [out], 0.13 + 2 * size(out) * CY)

    def dma(dst, src, rd, wr, sem, lat):
        return add("Y", lambda g, T: g.sync.dma_start(dst(T), src(T)), rd, wr, 0.1, sem=sem, amt=16, kind="dma", lat=lat)

    def send(mate, dst, src, here, sem, net, dep=()):
        i = add("G", (mate, dst, src, sem), [src], [], COST["send"], dep=dep, kind="send")
        add("N", None, [], [here], 0.0, sem=sem, amt=NE, dep=(i,), kind="net", lat=net)
        return i

    def send_shelf(r, cuts, net, dep=()):
        for h, (a, b) in enumerate(cuts):
            far = A("sh%d" % (r + 1), a, b)
            send(rank ^ ROUNDS[r], far, A("sh", a, b), far, "s%d_%d" % (r, a // 1024), net + 3 * h, dep)

    dma(lambda T: T.uin[:], lambda T: T.units[:], [], [A("uin")], "ldu", 2.5)
    for h in range(4):
        a, b = 1024 * h, 1024 * h + 1024
        dma(lambda T, a=a, b=b: T.sh[:, a:b], lambda T, a=a, b=b: T.shelf[:, a:b], [], [A("sh", a, b)], "lds%d" % h, 3.5 + 1.5 * h)
    iota(A("ip"), [[1, 1]], 0, 1)
    iota(A("im"), [[1, 128]], 0, 0)
    iota(A("jj"), [[0, 64], [1, 16]], 0, 0)
    iota(A("tie"), [[-1, 256]], 255, 0, True)
    send_shelf(0, [(0, 1024), (1024, 2048), (2048, 3072)], 8.0)
    cp(FC(0), A("ip"))
    ts(A("ii", 0, 1), A("ip"), 4, None, OP.arith_shift_right)
    cp(FC(1), A("ii", 0, 1))
    ts(A("ii", 1, 2), A("ip"), 15, None, OP.bitwise_and)
    cp(FC(2), A("ii", 1, 2))
    ts(A("mg"), A("im"), 4, None, OP.arith_shift_right)
    ts(A("bf"), A("mg"), FC(1), None, OP.is_equal)
    ts(A("gef"), A("im"), FC(0), None, OP.is_ge)
    tt(A("trif"), A("bf"), A("gef"), OP.mult)
    ts(A("idf"), A("im"), FC(0), None, OP.is_equal)
    ts(MH(0), A("trif"), 1.0, None, OP.mult)
    ts(MH(1), A("idf"), 32.0, None, OP.mult)
    ts(MH(2), A("idf"), 1.0, None, OP.mult)
    ts(A("half"), A("im", 0, 8), 0.0, 0.5, OP.mult, OP.add)
    ts(A("one"), A("im"), 0.0, 1.0, OP.mult, OP.add)
    ts(DA(0), A("idf"), -2048.0, None, OP.mult)
    for k, src, f in ((0, "idf", -4096.0), (1, "idf", -8388608.0 + 65536.0), (6, "bf", 1.0), (7, "bf", -1.0), (8, "bf", 256.0),
                      (9, "bf", -256.0), (10, "bf", 4096.0), (11, "bf", -4096.0), (12, "idf", 1.0)):
        act(MB(k), A(src), AF.Copy, scale=f)
    add("V", lambda g, T: g.vector.memset(T.ones[:], 1.0), [], [A("ones")], vcost(128))
    add("V", lambda g, T: g.vector.memset(T.mhalf[:], -0.5), [], [A("mhalf")], vcost(64))
    ts(A("rm"), A("jj"), 0, None, OP.is_gt)
    ts(A("bg"), A("jj"), 0, 256.0, OP.is_equal, OP.mult)
    ts(A("dm"), A("jj", 0, 64), FC(2), None, OP.is_equal)
    for t in range(4):
        ts(A("ii", 2 + t, 3 + t), A("ip"), 8 >> t, None, OP.bitwise_and)
        ts(FC(3 + t), A("ii", 2 + t, 3 + t), 0, None, OP.is_equal)
        ts(FC(7 + t), FC(3 + t), -16384.0, 8192.0, OP.mult, OP.add)
        ts(FC(11 + t), FC(3 + t), 65536.0, -8388608.0 + 65536.0, OP.mult, OP.add)
        ts(FC(15 + t), FC(3 + t), -1.0, None, OP.mult)
        ts(MH(3 + t), A("trif"), FC(3 + t), None, OP.mult)
        ts(MH(7 + t), A("trif"), FC(15 + t), None, OP.mult)
        ts(MH(11 + t), A("idf"), FC(3 + t), 32.0, OP.mult, OP.mult)
        ts(MH(15 + t), A("idf"), FC(3 + t), -32.0, OP.mult, OP.mult)
        act(MB(2 + t), A("idf"), AF.Copy, scale=FC(11 + t))
    ts(A("wa"), A("bf"), FC(2), 0.5, OP.mult, OP.mult)
    h1 = A("half", 0, 1)

    def pcol(k):
        return A("p7", 500 + k, 501 + k)
    mm([(pcol(0), MH(0), h1)])
    ts(A("bs", 0, 1), pcol(0), 4096.0, 788480.0, OP.mult, OP.add)
    ts(A("bt", 0, 1), A("bs", 0, 1), P2, -4095.0 / 8192, OP.mult, OP.add)
    for t in range(4):
        mm([(pcol(1 + t), MH(0), h1), (pcol(1 + t), MH(3 + t), h1)])
    ts(A("bs", 1, 5), A("p7", 501, 505), 4096.0, 788480.0, OP.mult, OP.add)
    ts(A("bt", 1, 5), A("bs", 1, 5), P2, -4095.0 / 8192, OP.mult, OP.add)
    ts(A("xc"), A("uin"), -2048.0, None, OP.add)
    a0 = 264 if rank < (rank ^ ROUNDS[0]) else 7
    ts(A("vs", a0, a0 + 1), A("ip"), 0.0, -2048.0, OP.mult, OP.add)

    def columns(c, lo, hi, k, pre, late, xpt):
        n = hi - lo
        x, w, xp = A("p%d" % (2 * c), 0, n), A("p%d" % (2 * c + 1), 0, n), A("p%d" % (2 * c), 384, 384 + n)
        tb = A("tb", lo, hi)
        i = mm(pre(x), last=not late(x))
        if late(x):
            i = mm(late(x), first=False, dep=(i,))
        i = mm(pre(w) + late(w), last=False, dep=(i,))
        ts(tb, x, P2, A("bt", k, k + 1), OP.mult, OP.add)
        mm([(w, MB(0), tb)], first=False, dep=(i,))
        mm(xpt(xp))
        act(A("sq", lo, hi), w, AF.Square, bias=A("bs", k, k + 1))
        tt(A("yb", lo, hi), A("sq", lo, hi), xp, OP.add)
        ts(A("cb", lo, hi), A("yb", lo, hi), 5, 4095, OP.arith_shift_right, OP.bitwise_and)
        cp(A("c16", lo, hi), A("cb", lo, hi))

    def gather_scan(parts):
        for (a, b, win) in parts:
            gath(A("gb", 16 * a, 16 * b), A(win), A("c16", a, b), "S")
        for (a, b, win) in parts:
            m = 16 * (b - a)
            scan(A("mx", 16 * a, 16 * b), A("rm", 0, m), A("gb", 16 * a, 16 * b), OP.mult, OP.max)
            scan(A("mn", 16 * a, 16 * b), A("bg", 0, m), A("gb", 16 * a, 16 * b), OP.max, OP.min)

    def ends(nm, a, b):
        return A(nm, 16 * a + 15, 16 * b, 16)

    for r, m in enumerate(ROUNDS):
        mate = rank ^ m
        low = rank < mate
        for c, (lo, hi) in enumerate(BCH):
            n = hi - lo
            stg[0] = 1000 * r + c
            xs = A("xc", lo, hi)
            columns(c, lo, hi, 0, lambda x: [(x, MH(0), xs), (x, DA(r), A("one", 0, n))], lambda x: [],
                    lambda x: [(x, MH(1), xs), (x, MB(1), A("ones", 0, n))])
            st = n // SUBS // 2 * 2
            cut = [lo + s * st for s in range(SUBS)] + [hi]
            gather_scan([(cut[s], cut[s + 1], "sh") for s in range(SUBS)])
            mx, mn = ends("mx", lo, hi), ends("mn", lo, hi)
            kp, vp = A("p%d" % (2 * c + 1), 128, 128 + n), A("p%d" % (2 * c + 1), 256, 256 + n)
            mm([(kp, MB(8 if low else 9), mx), (kp, MB(9 if low else 8), mn), (kp, MB(12), A("tie", lo, hi))])
            mm([(vp, MB(10), mx), (vp, MB(11), mn), (vp, MH(2), xs)])
            tt(A("kd", lo, hi), kp, A("dm", 0, n), OP.mult)
            cp(A("ksb", lo, hi), kp)
            scan(A("kc", lo, hi), A("rm", 0, n), A("kd", lo, hi), OP.mult, OP.add, 1)
            ts(A("vu", lo, hi), vp, 2048.0, None, OP.add)
        stg[0] = 1000 * r + 20
        for j in range(16):
            kcol = A("kc", 16 * j + 15, 16 * j + 16)
            if j < NS:
                act(A("trash", 256 * (j % 4), 256 * (j % 4) + 256), A("ksb"), AF.Sign, bias=kcol, scale=-1.0, acc=A("acc", j, j + 1))
            else:
                ts(A("cmp", 256 * j, 256 * j + 256), A("ksb"), kcol, None, OP.is_gt)
                scan(A("cs", 256 * j, 256 * j + 256), A("ones"), A("cmp", 256 * j, 256 * j + 256), OP.mult, OP.add)
        ts(A("rl", 16 * r + NS, 16 * r + 16), A("cs", 256 * NS + 255, 4096, 256), 1.0, None, OP.mult)
        ts(A("rl", 16 * r, 16 * r + NS), A("acc", 0, NS), -0.5, 127.5, OP.mult, OP.add)
        rl = A("rl", 16 * r, 16 * r + 16)
        v0 = 272 * r + 8
        vw = A("vs", v0, v0 + 256)
        add("V", lambda g, T, vw=vw, rl=rl: g.vector.tensor_copy(ap(T, vw).indirect(ap(T, rl)), T.vu[:]), [rl, A("vu")], [vw], 0.05 + 256 * CY * 3)
        mine = v0 + (0 if low else 128)
        f0 = 144 * r
        x0 = f0 + (1 if low else 0)
        far = A("vf", f0, f0 + 129)
        iv = send(mate, far, A("vs", v0 + 128, v0 + 257) if low else A("vs", v0 - 1, v0 + 128), far, "v%d" % r, COST["net"])
        mv, fv = A("vs", mine, mine + 128), A("vf", x0, x0 + 128)
        stg[0] = 1000 * r + 21
        if r == 0:
            send_shelf(0, [(3072, 4096)], 6.0, (iv,))
        if r < 2:
            send_shelf(r + 1, [(0, 4096)], 16.0, (len(ops) - 2,))
        for c, (a, b) in enumerate(TCH):
            n = b - a
            stg[0] = 1000 * r + 100 + c
            L, H = A("oi", 2 * a, 2 * a + n), A("oi", 2 * a + n, 2 * b)
            cL, cH = A("oc", 2 * a, 2 * a + n), A("oc", 2 * a + n, 2 * b)
            ow, fr = (L, H) if low else (H, L)
            cow, cfr = (cL, cH) if low else (cH, cL)
            ts(ow, A("vs", mine + a, mine + b), 4095, None, OP.bitwise_and)
            ts(cow, ow, -2048.0, None, OP.add)
            ts(fr, A("vf", x0 + a, x0 + b), 4095, None, OP.bitwise_and)
            ts(cfr, fr, -2048.0, None, OP.add)
            d = A("d", a, b)
            tt(d, H, L, OP.subtract)
            ts(d, d, 4095, None, OP.bitwise_and)
            ts(A("rr", a, b), d, -2048.0, None, OP.add)
        stg[0] = 1000 * r + 100
        ac = A("ac", 4 * r + 2, 4 * r + 3)
        fa = f0 if low else f0 + 128
        cp(ac, A("vf", fa, fa + 1))
        ts(DA(3 + r), A("idf"), ac, None, OP.mult)
        stg[0] = 1000 * r + 103
        ts(A("qo"), mv, 12, None, OP.arith_shift_right)
        ts(A("qf"), fv, 12, None, OP.arith_shift_right)
        qL, qH = (A("qo"), A("qf")) if low else (A("qf"), A("qo"))
        tt(A("s0"), qL, qH, OP.is_gt)
        ts(A("s0"), A("s0"), 2.0, -1.0, OP.mult, OP.add)
        for t in range(4):
            stg[0] = 1000 * r + 103 + 4 * t
            ts(A("sg", 128 * t, 128 * t + 128), A("s0"), FC(7 + t), None, OP.mult)
        tt(A("tl", 0, 128), qL, qH, OP.is_lt)
        ts(A("tl", 128, 256), A("tl", 0, 128), -1.0, None, OP.add)
        if r == 2:
            ts(A("qi"), A("vu"), 12, None, OP.arith_shift_right)
            cp(A("qy"), A("qi"))
            dma(lambda T: T.yq[:], lambda T: T.qy[0:128:16, :], [A("qy")], [], "styq", 2.0)
        dL, dH = (DA(r), DA(3 + r)) if low else (DA(3 + r), DA(r))
        wL, wH = ("sh", "sh%d" % (r + 1)) if low else ("sh%d" % (r + 1), "sh")
        for t in range(4):
            for c, (a, b) in enumerate(TCH):
                n = b - a
                lo, mid, hi = 2 * a, 2 * a + n, 2 * b
                stg[0] = 1000 * r + 100 + 4 * t + c
                R, oc, one = A("rr", a, b), A("oc", lo, hi), A("one", 0, n)

                def lh(x):
                    return (x[0], x[1], x[1] + n, 1), (x[0], x[1] + n, x[1] + 2 * n, 1)
                columns(c, lo, hi, 1 + t,
                        lambda x: [(x, MH(0), oc), (lh(x)[0], dL, one), (lh(x)[1], dH, one)],
                        lambda x: [(lh(x)[0], MH(3 + t), R), (lh(x)[1], MH(7 + t), R)],
                        lambda x: [(x, MH(1), oc), (x, MB(2 + t), A("ones", 0, 2 * n)), (lh(x)[0], MH(11 + t), R), (lh(x)[1], MH(15 + t), R)])
                gather_scan([(lo, mid, wL), (mid, hi, wH)])
                q = A("p%d" % (2 * c + 1), 128, 128 + n)
                i = mm([(q, MB(12), A("mhalf", 0, n)), (q, MB(6), ends("mx", lo, mid)), (q, MB(7), ends("mn", lo, mid))], last=False)
                mm([(q, MB(7), ends("mx", mid, hi)), (q, MB(6), ends("mn", mid, hi))], first=False, dep=(i,))
                stg[0] += 4
                u, e = A("u", a, b), A("e", a, b)
                tt(u, q, A("sg", 128 * t + a, 128 * t + b), OP.mult)
                tt(e, A("d" if t == 0 else "e", a, b), u, OP.min)
                if t < 3:
                    ts(R, e, 0.0, -2048.0, OP.max, OP.add)
                    continue
                if r < 2:
                    act(A("sgn", a, b), e, AF.Sign, bias=0.5, acc=A("cnt", c, c + 1))
                r5, rL, rH = A("r5", a, b), A("r2", lo, mid), A("r2", mid, hi)
                ts(r5, e, 0.0, None, OP.max)
                tt(rL, r5, A("tl", a, b), OP.mult)
                tt(rH, r5, A("tl", 128 + a, 128 + b), OP.mult)
                tt(A("ns", lo, hi), A("oi", lo, hi), A("r2", lo, hi), OP.add)
                sL, sH = A("ns", lo, mid), A("ns", mid, hi)
                so, sf = (sL, sH) if low else (sH, sL)
                ts(A("nf", x0 + a, x0 + b), sf, 4095, None, OP.bitwise_and)
                ts(A("nx", mine + a, mine + b), so, 4095, None, OP.bitwise_and)
        stg[0] = 1000 * r + 200
        nw = A("nx", v0, v0 + 256)
        n0 = 144 * r
        if r < 2:
            pa = A("p0", 500, 501)
            cn = [(pa, A("wa"), A("cnt", c, c + 1)) for c in range(len(TCH))]
            mm(cn[-1:], first=False, dep=(mm(cn[:-1], last=False),))
            fcol = n0 if low else n0 + 128
            ts(A("nf", fcol, fcol + 1), pa, 7680.0, None, OP.add)
            ts(A("ac", 4 * r, 4 * r + 1), pa, 5632.0, None, OP.add)
            front, back = A("nx", v0 - 1, v0 + 128), A("nx", v0 + 128, v0 + 257)
            send(mate, front if low else back, A("nf", n0, n0 + 129), back if low else front, "n%d" % r, COST["net"])
            rcv = A("nx", v0 + 256, v0 + 257) if low else A("nx", v0 - 1, v0)
            asum = A("ac", 4 * r + 1, 4 * r + 2)
            tt(asum, A("ac", 4 * r, 4 * r + 1), rcv, OP.add)
            ts(DA(r + 1), A("idf"), asum, None, OP.mult)
            vn = 272 * (r + 1) + 8
            acol = A("vs", vn + 256, vn + 257) if rank < (rank ^ ROUNDS[r + 1]) else A("vs", vn - 1, vn)
            cp(acol, asum)
            for c, (lo, hi) in enumerate(BCH):
                stg[0] = 1000 * (r + 1) + c
                xs, rc = A("xc", lo, hi), A("rl", 16 * r + lo // 16, 16 * r + hi // 16)
                add("V", lambda g, T, xs=xs, rc=rc, nw=nw: g.vector.tensor_scalar(ap(T, xs), ap(T, nw).indirect(ap(T, rc)), -2048.0, None, OP.add),
                    [rc, nw], [xs], 0.05 + (hi - lo) * CY * COST["g"])
        else:
            front, back = A("nx", v0, v0 + 128), A("nx", v0 + 128, v0 + 256)
            send(mate, front if low else back, A("nf", x0, x0 + 128), back if low else front, "n%d" % r, COST["net"])
            for h in range(2):
                a, b = 128 * h, 128 * h + 128
                gath(A("yo", a, b), nw, A("rl", 16 * r + 8 * h, 16 * r + 8 * h + 8), "V")
                dma(lambda T, a=a, b=b: T.yu[:, a:b], lambda T, a=a, b=b: T.yo[:, a:b], [A("yo", a, b)], [], "styu%d" % h, 2.0)
    return ops


def schedule(ops):
    n = len(ops)
    succ = [[] for _ in ops]
    for i, o in enumerate(ops):
        for j in o["d"]:
            succ[j].append(i)

    def lat(j, i):
        if ops[j]["lat"] is not None:
            return ops[j]["lat"]
        return COST["self"] if ops[j]["e"] == ops[i]["e"] else COST["lat"]
    pr = [0.0] * n
    sg = [9999 if o["s"] is None else o["s"] for o in ops]
    for i in range(n - 1, -1, -1):
        pr[i] = ops[i]["c"] + max([pr[s] + lat(i, s) for s in succ[i]] + [0.0])
        if ops[i]["s"] is None:
            sg[i] = min([sg[x] for x in succ[i]] + [9999])
    cnt = [len(o["d"]) for o in ops]
    ready, start = [0.0] * n, [0.0] * n
    free, avail, order = {}, {}, []
    for i in range(n):
        if cnt[i] == 0:
            avail.setdefault(ops[i]["e"], []).append(i)
    while len(order) < n:
        best = None
        for e, lst in avail.items():
            if not lst:
                continue
            f = free.get(e, 0.0)
            s0 = max(f, min(ready[k] for k in lst))
            if e == "N":
                i = min(lst, key=lambda k: ready[k])
                s = ready[i]
            else:
                i = min((k for k in lst if ready[k] <= s0 + WIN), key=lambda k: (ops[k]["c"] > COST["long"], sg[k], -pr[k]))
                s = max(f, ready[i])
            if best is None or s < best[0]:
                best = (s, i, e)
        s, i, e = best
        avail[e].remove(i)
        start[i] = s
        end = s + ops[i]["c"]
        if e != "N":
            free[e] = end
        order.append(i)
        for k in succ[i]:
            ready[k] = max(ready[k], end + lat(i, k))
            cnt[k] -= 1
            if cnt[k] == 0:
                avail.setdefault(ops[k]["e"], []).append(k)
    return order, start


def rank_program(g, core, T, topo):
    rank = T.rank_of(core)
    if rank is None:
        return
    ops = build(rank)
    order, start = schedule(ops)
    queue = {"P": g.tensor, "V": g.vector, "S": g.scalar, "G": g, "Y": g.sync}
    own = {"P": "eP", "V": "eV", "S": "eS", "G": "eG"}
    known = {e: {} for e in queue}
    after = {}
    count, sent = {}, 0
    for i in order:
        o = ops[i]
        e = o["e"]
        if e == "N":
            o["at"] = (o["sem"], o["amt"])
            after[i] = {o["sem"]: o["amt"]}
            continue
        kn = known[e]
        need = [ops[j]["at"] + (j,) for j in o["d"]
                if (e, ops[j]["e"]) != ("P", "P") and kn.get(ops[j]["at"][0], 0) < ops[j]["at"][1]]
        for (s, v, j) in need:
            if not any(j2 != j and after[j2].get(s, 0) >= v and (s2 != s or v2 > v or j2 > j) for (s2, v2, j2) in need):
                queue[e].wait_ge(T.sem[s], v)
        for (s, v, j) in need:
            for s2, v2 in after[j].items():
                kn[s2] = max(kn.get(s2, 0), v2)
        if o["k"] == "send":
            mate, dst, src, sem = o["fn"]
            to = T.cores[mate]
            rid, pid, ring = topo.addr(to)
            eng = topo.engines(core, to)[-NE:]
            g.remote_dma(T[dst[0]][:, dst[1]:dst[2]], T[src[0]][:, src[1]:src[2]], T.sem[sem], T.sem.lsem, pid, rid, sum(1 << x for x in eng))
            sent += len(eng)
            after[i] = dict(kn)
            o["at"] = ("lsem", 0)
            continue
        s = o["sem"] or own[e]
        o["fn"](g, T).then_inc(T.sem[s], o["amt"])
        count[s] = count.get(s, 0) + o["amt"]
        o["at"] = (s, count[s])
        after[i] = dict(kn)
        after[i][s] = count[s]
    for s, v in sorted(count.items()):
        if known["G"].get(s, 0) < v:
            g.wait_ge(T.sem[s], v)
    g.wait_ge(T.sem.lsem, sent)
